import numpy as np
import ml_dtypes

BF16 = ml_dtypes.bfloat16


def bf(x):
    return np.asarray(x, np.float32).astype(BF16)


def f32(x):
    return np.asarray(x, np.float32)


def f64(x):
    return np.asarray(x).astype(np.float64)


def striped(idx):
    return np.tile(idx.reshape(-1, 16).T, (8, 1))


def rows(idx, k):
    return np.tile(idx, (k, 1))


def look(tab, idx):
    return np.take_along_axis(f64(tab), rows(idx, len(tab)), axis=1)


K, S, V, N, M = 128, 2048, 2048, 2048, 512


def setup_inputs():
    return {"tab": f32(np.random.standard_normal((2, K, S))), "w": bf(np.random.standard_normal((K, M)) / np.sqrt(K)), "b": f32(0.5 * np.random.standard_normal((M, 1))), "offs": striped(np.random.permutation(S)[:N])}


def reference(tab, w, b, offs):
    idx = offs[:16].T.reshape(-1)
    x = ((look(tab[0], idx) - 0.125) * 1.5) * (np.tanh(look(tab[1], idx)))
    return np.maximum(f64(w).T @ x + f64(b), 0.0)

@@ -1,0 +1,72 @@
+import concourse.mybir as mybir
+from concourse.masks import make_identity
+
+ACT = mybir.ActivationFunctionType
+ALU = mybir.AluOpType
+BF16, F32, U16 = mybir.dt.bfloat16, mybir.dt.float32, mybir.dt.uint16
+
+ROWS, PLACES, ENTRIES, UNITS = 128, 2048, 2048, 512
+PIECE = 512
+BLOCK = 128
+
+FLOPS = 2 * ROWS * UNITS * ENTRIES
+
+
+def tile_lookup_vg_nrmtanh_relu_kernel(tc, tab, w, b, offs, out):
+    nc = tc.nc
+    blocks = UNITS // BLOCK
+    list_columns = PIECE // 16
+
+    with (
+        tc.tile_pool(name="held", bufs=1) as held,
+        tc.tile_pool(name="pieces", bufs=2) as pieces,
+        tc.tile_pool(name="results", bufs=8) as results,
+        tc.psum_pool(name="psum", bufs=6) as psum,
+        tc.psum_pool(name="psum_bias", bufs=1) as psum_bias,
+    ):
+        offsets = held.tile([128, ENTRIES // 16], U16)
+        values = held.tile([ROWS, PLACES], F32)
+        gates = held.tile([ROWS, PLACES], F32)
+        nc.sync.dma_start(offsets[:], offs)
+        nc.sync.dma_start(values[:], tab[0])
+        nc.sync.dma_start(gates[:], tab[1])
+
+        weights = held.tile([ROWS, UNITS], BF16)
+        nc.sync.dma_start(weights[:], w)
+
+        bias_rows = held.tile([128, BLOCK], F32)
+        nc.vector.memset(bias_rows[:], 0.0)
+        nc.sync.dma_start(bias_rows[0:blocks, :], b.rearrange("(k p) one -> k (p one)", p=BLOCK))
+        identity = held.tile([128, 128], F32)
+        make_identity(nc, identity[:])
+        bias_columns = psum_bias.tile([BLOCK, 128], F32)
+        nc.tensor.transpose(bias_columns[:], bias_rows[:], identity[:])
+        bias = held.tile([BLOCK, blocks], F32)
+        nc.vector.tensor_copy(bias[:], bias_columns[:, 0:blocks])
+
+        for piece in range(ENTRIES // PIECE):
+            entries = slice(piece * PIECE, (piece + 1) * PIECE)
+            places = offsets[:, piece * list_columns : (piece + 1) * list_columns]
+
+            scaled = pieces.tile([ROWS, PIECE], F32)
+            nc.vector.tensor_scalar(
+                scaled[:], values[:].indirect(places), 0.125, 1.5, ALU.subtract, ALU.mult
+            )
+            opened = pieces.tile([ROWS, PIECE], F32)
+            nc.scalar.activation(opened[:], gates[:].indirect(places), ACT.Tanh)
+            x = pieces.tile([ROWS, PIECE], BF16)
+            nc.vector.tensor_tensor(x[:], scaled[:], opened[:], ALU.mult)
+
+            for k in range(blocks):
+                units = slice(k * BLOCK, (k + 1) * BLOCK)
+                product = psum.tile([BLOCK, PIECE], F32)
+                nc.tensor.matmul(product[:], weights[:, units], x[:], start=True, stop=True)
+
+                result = results.tile([BLOCK, PIECE], F32)
+                if k % 2 == 0:
+                    nc.scalar.activation(result[:], product[:], ACT.Relu, bias=bias[:, k : k + 1])
+                else:
+                    nc.vector.tensor_scalar(
+                        result[:], product[:], bias[:, k : k + 1], 0.0, ALU.add, ALU.max
+                    )
+                nc.sync.dma_start(out[units, entries], result[:])

@@ -19,11 +19,16 @@ def tile_lookup_vg_nrmtanh_relu_kernel(tc, tab, w, b, offs, out):
 
     with (
         tc.tile_pool(name="held", bufs=1) as held,
-        tc.tile_pool(name="pieces", bufs=2) as pieces,
+        tc.tile_pool(name="pieces", bufs=4) as pieces,
         tc.tile_pool(name="results", bufs=8) as results,
-        tc.psum_pool(name="psum", bufs=6) as psum,
+        tc.psum_pool(name="psum", bufs=7) as psum,
         tc.psum_pool(name="psum_bias", bufs=1) as psum_bias,
     ):
+        zeros = held.tile([128, 1], F32)
+        nc.vector.memset(zeros[:], 0.0)
+        warmed = held.tile([128, 1], F32)
+        nc.scalar.activation(warmed[:], zeros[:], ACT.Tanh)
+
         offsets = held.tile([128, ENTRIES // 16], U16)
         values = held.tile([ROWS, PLACES], F32)
         gates = held.tile([ROWS, PLACES], F32)
@@ -36,7 +41,7 @@ def tile_lookup_vg_nrmtanh_relu_kernel(tc, tab, w, b, offs, out):
 
         bias_rows = held.tile([128, BLOCK], F32)
         nc.vector.memset(bias_rows[:], 0.0)
-        nc.sync.dma_start(bias_rows[0:blocks, :], b.rearrange("(k p) one -> k (p one)", p=BLOCK))
+        nc.scalar.dma_start(bias_rows[0:blocks, :], b.rearrange("(k p) one -> k (p one)", p=BLOCK))
         identity = held.tile([128, 128], F32)
         make_identity(nc, identity[:])
         bias_columns = psum_bias.tile([BLOCK, 128], F32)

@@ -6,7 +6,6 @@ ALU = mybir.AluOpType
 BF16, F32, U16 = mybir.dt.bfloat16, mybir.dt.float32, mybir.dt.uint16
 
 ROWS, PLACES, ENTRIES, UNITS = 128, 2048, 2048, 512
-PIECE = 512
 BLOCK = 128
 
 FLOPS = 2 * ROWS * UNITS * ENTRIES
@@ -15,11 +14,12 @@ FLOPS = 2 * ROWS * UNITS * ENTRIES
 def tile_lookup_vg_nrmtanh_relu_kernel(tc, tab, w, b, offs, out):
     nc = tc.nc
     blocks = UNITS // BLOCK
-    list_columns = PIECE // 16
 
     with (
         tc.tile_pool(name="held", bufs=1) as held,
-        tc.tile_pool(name="pieces", bufs=4) as pieces,
+        tc.tile_pool(name="values_ahead", bufs=2) as values_ahead,
+        tc.tile_pool(name="gates_ahead", bufs=4) as gates_ahead,
+        tc.tile_pool(name="operands", bufs=4) as operands,
         tc.tile_pool(name="results", bufs=8) as results,
         tc.psum_pool(name="psum", bufs=7) as psum,
         tc.psum_pool(name="psum_bias", bufs=1) as psum_bias,
@@ -29,19 +29,11 @@ def tile_lookup_vg_nrmtanh_relu_kernel(tc, tab, w, b, offs, out):
         warmed = held.tile([128, 1], F32)
         nc.scalar.activation(warmed[:], zeros[:], ACT.Tanh)
 
-        offsets = held.tile([128, ENTRIES // 16], U16)
-        values = held.tile([ROWS, PLACES], F32)
-        gates = held.tile([ROWS, PLACES], F32)
-        nc.sync.dma_start(offsets[:], offs)
-        nc.sync.dma_start(values[:], tab[0])
-        nc.sync.dma_start(gates[:], tab[1])
-
-        weights = held.tile([ROWS, UNITS], BF16)
-        nc.sync.dma_start(weights[:], w)
-
+        loaded = held.tile([blocks, BLOCK], F32)
+        nc.sync.dma_start(loaded[:], b.rearrange("(k p) one -> k (p one)", p=BLOCK))
         bias_rows = held.tile([128, BLOCK], F32)
         nc.vector.memset(bias_rows[:], 0.0)
-        nc.scalar.dma_start(bias_rows[0:blocks, :], b.rearrange("(k p) one -> k (p one)", p=BLOCK))
+        nc.vector.tensor_copy(bias_rows[0:blocks, :], loaded[:])
         identity = held.tile([128, 128], F32)
         make_identity(nc, identity[:])
         bias_columns = psum_bias.tile([BLOCK, 128], F32)
@@ -49,26 +41,38 @@ def tile_lookup_vg_nrmtanh_relu_kernel(tc, tab, w, b, offs, out):
         bias = held.tile([BLOCK, blocks], F32)
         nc.vector.tensor_copy(bias[:], bias_columns[:, 0:blocks])
 
-        for piece in range(ENTRIES // PIECE):
-            entries = slice(piece * PIECE, (piece + 1) * PIECE)
-            places = offsets[:, piece * list_columns : (piece + 1) * list_columns]
+        offsets = held.tile([128, ENTRIES // 16], U16)
+        values = held.tile([ROWS, PLACES], F32)
+        gates = held.tile([ROWS, PLACES], F32)
+        nc.sync.dma_start(offsets[:], offs)
+        nc.sync.dma_start(gates[:], tab[1])
+        nc.sync.dma_start(values[:], tab[0])
 
-            scaled = pieces.tile([ROWS, PIECE], F32)
+        weights = held.tile([ROWS, UNITS], BF16)
+        nc.sync.dma_start(weights[:], w)
+
+        start = 0
+        for width in (256, 512, 512, 512, 256):
+            entries = slice(start, start + width)
+            places = offsets[:, start // 16 : (start + width) // 16]
+            start += width
+
+            scaled = values_ahead.tile([ROWS, width], F32)
             nc.vector.tensor_scalar(
                 scaled[:], values[:].indirect(places), 0.125, 1.5, ALU.subtract, ALU.mult
             )
-            opened = pieces.tile([ROWS, PIECE], F32)
+            opened = gates_ahead.tile([ROWS, width], F32)
             nc.scalar.activation(opened[:], gates[:].indirect(places), ACT.Tanh)
-            x = pieces.tile([ROWS, PIECE], BF16)
+            x = operands.tile([ROWS, width], BF16)
             nc.vector.tensor_tensor(x[:], scaled[:], opened[:], ALU.mult)
 
             for k in range(blocks):
                 units = slice(k * BLOCK, (k + 1) * BLOCK)
-                product = psum.tile([BLOCK, PIECE], F32)
+                product = psum.tile([BLOCK, width], F32)
                 nc.tensor.matmul(product[:], weights[:, units], x[:], start=True, stop=True)
 
-                result = results.tile([BLOCK, PIECE], F32)
-                if k % 2 == 0:
+                result = results.tile([BLOCK, width], F32)
+                if start < ENTRIES - 256 or k % 2 == 0:
                     nc.scalar.activation(result[:], product[:], ACT.Relu, bias=bias[:, k : k + 1])
                 else:
                     nc.vector.tensor_scalar(

import concourse.mybir as mybir
from concourse.masks import make_identity

ACT = mybir.ActivationFunctionType
ALU = mybir.AluOpType
BF16, F32, U16 = mybir.dt.bfloat16, mybir.dt.float32, mybir.dt.uint16

ROWS, PLACES, ENTRIES, UNITS = 128, 2048, 2048, 512
BLOCK = 128

FLOPS = 2 * ROWS * UNITS * ENTRIES


def tile_lookup_vg_nrmtanh_relu_kernel(tc, tab, w, b, offs, out):
    nc = tc.nc
    blocks = UNITS // BLOCK

    with (
        tc.tile_pool(name="held", bufs=1) as held,
        tc.tile_pool(name="values_ahead", bufs=2) as values_ahead,
        tc.tile_pool(name="gates_ahead", bufs=4) as gates_ahead,
        tc.tile_pool(name="operands", bufs=4) as operands,
        tc.tile_pool(name="results", bufs=8) as results,
        tc.psum_pool(name="psum", bufs=7) as psum,
        tc.psum_pool(name="psum_bias", bufs=1) as psum_bias,
    ):
        zeros = held.tile([128, 1], F32)
        nc.vector.memset(zeros[:], 0.0)
        warmed = held.tile([128, 1], F32)
        nc.scalar.activation(warmed[:], zeros[:], ACT.Tanh)

        loaded = held.tile([blocks, BLOCK], F32)
        nc.sync.dma_start(loaded[:], b.rearrange("(k p) one -> k (p one)", p=BLOCK))
        bias_rows = held.tile([128, BLOCK], F32)
        nc.vector.memset(bias_rows[:], 0.0)
        nc.vector.tensor_copy(bias_rows[0:blocks, :], loaded[:])
        identity = held.tile([128, 128], F32)
        make_identity(nc, identity[:])
        bias_columns = psum_bias.tile([BLOCK, 128], F32)
        nc.tensor.transpose(bias_columns[:], bias_rows[:], identity[:])
        bias = held.tile([BLOCK, blocks], F32)
        nc.vector.tensor_copy(bias[:], bias_columns[:, 0:blocks])

        offsets = held.tile([128, ENTRIES // 16], U16)
        values = held.tile([ROWS, PLACES], F32)
        gates = held.tile([ROWS, PLACES], F32)
        nc.sync.dma_start(offsets[:], offs)
        nc.sync.dma_start(gates[:], tab[1])
        nc.sync.dma_start(values[:], tab[0])

        weights = held.tile([ROWS, UNITS], BF16)
        nc.sync.dma_start(weights[:], w)

        start = 0
        for width in (256, 512, 512, 512, 256):
            entries = slice(start, start + width)
            places = offsets[:, start // 16 : (start + width) // 16]
            start += width

            scaled = values_ahead.tile([ROWS, width], F32)
            nc.vector.tensor_scalar(
                scaled[:], values[:].indirect(places), 0.125, 1.5, ALU.subtract, ALU.mult
            )
            opened = gates_ahead.tile([ROWS, width], F32)
            nc.scalar.activation(opened[:], gates[:].indirect(places), ACT.Tanh)
            x = operands.tile([ROWS, width], BF16)
            nc.vector.tensor_tensor(x[:], scaled[:], opened[:], ALU.mult)

            for k in range(blocks):
                units = slice(k * BLOCK, (k + 1) * BLOCK)
                product = psum.tile([BLOCK, width], F32)
                nc.tensor.matmul(product[:], weights[:, units], x[:], start=True, stop=True)

                result = results.tile([BLOCK, width], F32)
                if start < ENTRIES - 256 or k % 2 == 0:
                    nc.scalar.activation(result[:], product[:], ACT.Relu, bias=bias[:, k : k + 1])
                else:
                    nc.vector.tensor_scalar(
                        result[:], product[:], bias[:, k : k + 1], 0.0, ALU.add, ALU.max
                    )
                nc.sync.dma_start(out[units, entries], result[:])
